import numpy as np
import ml_dtypes


def mxq(x, axis, fmt="e4m3"):
    dtype, down = {"e4m3": (ml_dtypes.float8_e4m3fn, 7), "e5m2": (ml_dtypes.float8_e5m2, 14)}[fmt]
    v = np.moveaxis(np.asarray(x, np.float32).astype(ml_dtypes.bfloat16).astype(np.float64), axis, -1)
    blocks = v.reshape(v.shape[:-1] + (-1, 32))
    amax = np.abs(blocks).max(-1, keepdims=True)
    byte = np.maximum(np.where(amax > 0, np.frexp(amax)[1] - 1 + 127, 0) - down, 1)
    scale = np.exp2(byte - 127.0)
    codes = (blocks / scale).astype(np.float32).astype(dtype).astype(np.float64)
    return np.moveaxis((codes * scale).reshape(v.shape), -1, axis)


WIDE = False


def mx_kscale(k):
    if not WIDE:
        return np.ones(k)
    levels = np.array([10, -10, 5, -5, 0])
    if k % 512:
        return np.exp2(np.random.permutation(np.resize(levels, k // 32))).repeat(32)
    a = np.empty((k // 512, 16))
    for p in range(k // 512):
        a[p, :8] = np.random.permutation(np.resize(levels, 8))
        for g in range(8):
            far = levels[np.abs(levels - a[p, g]) >= 10]
            a[p, g + 8] = far[np.random.randint(len(far))]
    return np.exp2(a.ravel()).repeat(32)


BF16 = ml_dtypes.bfloat16


def bf(x):
    return np.asarray(x, np.float32).astype(BF16)


def f64(x):
    return np.asarray(x).astype(np.float64)

E4M3FN = np.array([(-1.0 if i & 128 else 1.0) * ((1.0 + (i & 7) / 8.0) * 2.0 ** (((i >> 3) & 15) - 7) if i & 120 else (i & 7) * 2.0 ** -9) for i in range(256)])


def e4m3fn_bytes(y):
    return np.clip(np.asarray(y, np.float64), -448.0, 448.0).astype(np.float32).astype(ml_dtypes.float8_e4m3fn).view(np.uint8)


def e4m3fn_values(b):
    return E4M3FN[b]


T, K, N, B = 1024, 2048, 1024, 128


def setup_inputs():
    s = mx_kscale(K)
    mom = np.random.standard_normal((T, K)) * s
    basis = np.random.standard_normal((K, N)) / np.sqrt(K) / s[:, None]
    mom_scale = (np.abs(mom).reshape(T, K // B, B).max(axis=2) / 448.0).astype(np.float32)
    basis_scale = (np.abs(basis).reshape(K // B, B, N // B, B).max(axis=(1, 3)) / 448.0).astype(np.float32)
    return {"mom_bytes": e4m3fn_bytes(mom / np.repeat(f64(mom_scale), B, axis=1)),
            "mom_scale": mom_scale,
            "basis_bytes": e4m3fn_bytes(basis / np.repeat(np.repeat(f64(basis_scale), B, axis=0), B, axis=1)),
            "basis_scale": basis_scale,
            "grad": bf(np.random.standard_normal((T, K)) * s),
            "accum": bf(0.25 + np.random.random((T, N)))}


def reference(mom_bytes, mom_scale, basis_bytes, basis_scale, grad, accum):
    mom = e4m3fn_values(mom_bytes) * np.repeat(f64(mom_scale), B, axis=1)
    basis = e4m3fn_values(basis_bytes) * np.repeat(np.repeat(f64(basis_scale), B, axis=0), B, axis=1)
    bq = mxq(basis, 0, "e4m3")
    r = mxq(mom, 1, "e4m3") @ bq
    h = mxq(f64(grad), 1, "e4m3") @ bq
    new_accum = f64(accum) + h * h
    step = r / np.sqrt(new_accum)
    return step, new_accum

from contextlib import ExitStack

import concourse.mybir as mybir
from concourse.masks import make_identity

T, K, N, B = 1024, 2048, 1024, 128
FLOPS = 2 * 2 * T * K * N

F32 = mybir.dt.float32
BF16 = mybir.dt.bfloat16
U32 = mybir.dt.uint32
U8 = mybir.dt.uint8
FP8 = mybir.dt.float8_e4m3fn
FP8X4 = mybir.dt.float8_e4m3fn_x4
MULT = mybir.AluOpType.mult
ADD = mybir.AluOpType.add
ACT = mybir.ActivationFunctionType

P = 128
PASSES = K // 512
TILES = T // P
HALF = 512


def tile_eigenbasis_adagrad_step_d2_kernel(tc, mom_bytes, mom_scale, basis_bytes, basis_scale, grad, accum, out_0, out_1):
    nc = tc.nc
    with ExitStack() as ctx:
        keep = ctx.enter_context(tc.tile_pool(name="keep", bufs=1))
        work = ctx.enter_context(tc.tile_pool(name="work", bufs=3))
        tps = ctx.enter_context(tc.psum_pool(name="tps", bufs=4))
        accs = ctx.enter_context(tc.psum_pool(name="accs", bufs=4))

        mom_rows = mom_bytes.rearrange("(p i) k -> p i k", i=TILES)
        grad_rows = grad.rearrange("(p i) k -> p i k", i=TILES)
        accum_rows = accum.rearrange("(p i) n -> p i n", i=TILES)
        step_rows = out_0.rearrange("(p i) n -> p i n", i=TILES)
        newacc_rows = out_1.rearrange("(p i) n -> p i n", i=TILES)

        ms = keep.tile([P, TILES, K // B], F32, name="ms")
        bs = keep.tile([P, PASSES, N // B], F32, name="bs")
        nc.scalar.dma_start(out=ms[:], in_=mom_scale.rearrange("(p i) j -> p i j", i=TILES))
        bsv = basis_scale.rearrange("(g q) b -> q g b", q=4)
        for q in range(4):
            nc.scalar.dma_start(out=bs[32 * q : 32 * q + 32, :, :], in_=bsv[q].partition_broadcast(32))

        basis_src = basis_bytes.rearrange("(g p t) n -> g p (t n)", p=P, t=4)
        bb = [keep.tile([P, 4 * N], U8, name="bb%d" % g) for g in range(PASSES)]
        mb, gr, ac = {}, {}, {}

        def load_m(js):
            t = keep.tile([P, len(js), K], U8, name="mb%d" % js[0])
            nc.sync.dma_start(out=t[:], in_=mom_rows[:, js[0] : js[0] + len(js), :])
            for n, i in enumerate(js):
                mb[i] = t[:, n, :]

        def load_g(js):
            t = keep.tile([P, len(js), K], BF16, name="gr%d" % js[0])
            nc.sync.dma_start(out=t[:], in_=grad_rows[:, js[0] : js[0] + len(js), :])
            for n, i in enumerate(js):
                gr[i] = t[:, n, :]

        def load_a(js):
            t = keep.tile([P, len(js), N], BF16, name="ac%d" % js[0])
            nc.sync.dma_start(out=t[:], in_=accum_rows[:, js[0] : js[0] + len(js), :])
            for n, i in enumerate(js):
                ac[i] = t[:, n, :]

        def load_b(g):
            nc.sync.dma_start(out=bb[g][:], in_=basis_src[g])

        load_m([0])
        load_b(0)
        load_g([0])
        load_b(1)
        load_m([1])
        load_b(2)
        load_g([1])
        load_b(3)
        load_m([2, 3])
        load_g([2, 3])
        load_m([4, 5])
        load_a([0, 1])
        load_g([4, 5])
        load_a([2, 3])
        load_m([6, 7])
        load_g([6, 7])
        load_a([4, 5])
        load_a([6, 7])

        ident = keep.tile([P, P], F32, name="ident")
        make_identity(nc, ident[:])

        bq, bqs = {}, {}
        def basis_ready(g, h, widen_on_vector=False):
            wide = work.tile([P, 4, HALF], BF16, name="bwide", bufs=3)
            for t in range(4):
                src = bb[g][:, t * N + h * HALF : t * N + h * HALF + HALF].bitcast(FP8)
                if widen_on_vector:
                    nc.vector.tensor_copy(out=wide[:, t, :], in_=src)
                else:
                    nc.scalar.copy(out=wide[:, t, :], in_=src)
            grp = work.tile([P, HALF, 4], BF16, name="bgrp", align_bytes=64, bufs=3)
            for b in range(4):
                nc.vector.tensor_scalar(
                    out=grp[:, 128 * b : 128 * b + 128, :],
                    in0=wide[:, :, 128 * b : 128 * b + 128].rearrange("p t n -> p n t"),
                    scalar1=bs[:, g, 4 * h + b : 4 * h + b + 1],
                    scalar2=None,
                    op0=MULT,
                )
            c = keep.tile([P, HALF], U32, name="bq%d%d" % (g, h), align_bytes=64)
            s = keep.tile([P, HALF], U8, name="bqs%d%d" % (g, h), align_bytes=64)
            nc.vector.quantize_mx(out=c[:].bitcast(FP8X4), scales=s[:], in_=grp[:].rearrange("p n t -> p (n t)"))
            bq[g, h], bqs[g, h] = c, s

        mwide = {}
        def widen_mom(i, on_scalar=False):
            w = work.tile([P, PASSES, 2, P, 2], BF16, name="mwide", align_bytes=64, bufs=3)
            for g in range(PASSES):
                for q in range(4):
                    k0 = 512 * g + B * q
                    nc.vector.tensor_scalar(
                        out=w[:, g, :, 32 * q : 32 * q + 32, :].rearrange("p u w e -> p w u e"),
                        in0=mb[i][:, k0 : k0 + B].bitcast(FP8).rearrange("p (w u e) -> p w u e", u=2, e=2),
                        scalar1=ms[:, i, 4 * g + q : 4 * g + q + 1],
                        scalar2=None,
                        op0=MULT,
                    )
            mwide[i] = w

        grp_of = {}
        def turn(kind, i, engines):
            if kind == "m":
                words = mwide[i][:].rearrange("p g u w e -> p (g u w e)").bitcast(F32)
            else:
                words = gr[i].bitcast(F32)
            grp = work.tile([P, PASSES, P, 4], BF16, name="grp", align_bytes=64, bufs=6)
            gw = grp[:].rearrange("p g r t -> p (g r t)").bitcast(F32).rearrange("p (g r u) -> p g r u", r=P, u=2)
            for half in range(2):
                bank = tps.tile([P, 2, 2, P], F32, name="tp")
                for gg in range(2):
                    for u in range(2):
                        g = 2 * half + gg
                        if kind == "m":
                            src = words[:, (2 * g + u) * P : (2 * g + u + 1) * P]
                        else:
                            src = words[:, 256 * g + u : 256 * (g + 1) : 2]
                        nc.tensor.transpose(bank[:, gg, u, :], src, ident[:])
                dst = gw[:, 2 * half : 2 * half + 2, :, :]
                srcb = bank[:].rearrange("p g u r -> p g r u")
                if engines[half] == "s":
                    nc.scalar.copy(out=dst, in_=srcb)
                else:
                    nc.vector.tensor_copy(out=dst, in_=srcb)
            grp_of[kind, i] = grp

        xq, xqs = {}, {}
        def quant(kind, i):
            c = work.tile([P, PASSES * P], U32, name=kind + "q", align_bytes=64, bufs=8)
            s = work.tile([P, PASSES * P], U8, name=kind + "qs", align_bytes=64, bufs=8)
            nc.vector.quantize_mx(out=c[:].bitcast(FP8X4), scales=s[:], in_=grp_of[kind, i][:].rearrange("p g r t -> p (g r t)"))
            xq[kind, i], xqs[kind, i] = c, s

        acc = {}
        def mx_pass(kind, i, h, g):
            if g == 0:
                acc[kind, i, h] = accs.tile([P, HALF], F32, name="acc")
            nc.tensor.matmul_mx(
                out=acc[kind, i, h][:],
                lhsT=xq[kind, i][:, g * P : (g + 1) * P].bitcast(FP8X4),
                lhsT_scale=xqs[kind, i][:, g * P : (g + 1) * P],
                rhs=bq[g, h][:].bitcast(FP8X4),
                rhs_scale=bqs[g, h][:],
                start=(g == 0),
                stop=(g == PASSES - 1),
            )

        def mx(kind, i, h):
            for g in range(PASSES):
                mx_pass(kind, i, h, g)

        def finish(i, h):
            sq = work.tile([P, HALF], F32, name="sq", bufs=3)
            nc.scalar.activation(out=sq[:], in_=acc["g", i, h][:], func=ACT.Square)
            na = work.tile([P, HALF], F32, name="na", bufs=4)
            cols = slice(h * HALF, h * HALF + HALF)
            nc.vector.tensor_tensor(out=na[:], in0=sq[:], in1=ac[i][:, cols], op=ADD)
            rs = work.tile([P, HALF], F32, name="rs", bufs=3)
            nc.scalar.activation(out=rs[:], in_=na[:], func=ACT.Abs_reciprocal_sqrt)
            st = work.tile([P, HALF], F32, name="st", bufs=4)
            nc.vector.tensor_tensor(out=st[:], in0=acc["m", i, h][:], in1=rs[:], op=MULT)
            nc.sync.dma_start(out=newacc_rows[:, i, cols], in_=na[:])
            nc.sync.dma_start(out=step_rows[:, i, cols], in_=st[:])

        def prep(i):
            widen_mom(i)
            turn("g", i, "ss")
            turn("m", i, "ss")
            quant("g", i)
            quant("m", i)

        turn("g", 3, "ss")
        quant("g", 3)
        turn("g", 1, "ss")
        quant("g", 1)
        widen_mom(0)
        turn("m", 0, "vs")
        quant("m", 0)
        basis_ready(0, 0)
        basis_ready(1, 0)
        turn("g", 0, "ss")
        quant("g", 0)
        widen_mom(2)
        widen_mom(3)
        basis_ready(3, 0, widen_on_vector=True)
        turn("g", 5, "ss")
        quant("g", 5)
        basis_ready(2, 0, widen_on_vector=True)
        widen_mom(5)
        mx("g", 0, 0)
        mx("m", 0, 0)
        finish(0, 0)
        turn("m", 2, "ss")
        quant("m", 2)
        turn("g", 7, "vs")
        quant("g", 7)
        turn("g", 2, "ss")
        quant("g", 2)
        turn("m", 3, "ss")
        quant("m", 3)
        mx("g", 2, 0)
        mx("m", 2, 0)
        finish(2, 0)
        mx("g", 3, 0)
        mx("m", 3, 0)
        finish(3, 0)
        widen_mom(4)
        turn("g", 6, "ss")
        quant("g", 6)
        basis_ready(2, 1)
        turn("g", 4, "ss")
        quant("g", 4)
        basis_ready(1, 1)
        basis_ready(0, 1, widen_on_vector=True)
        turn("m", 5, "ss")
        quant("m", 5)
        basis_ready(3, 1)
        mx("g", 5, 0)
        mx("m", 5, 0)
        finish(5, 0)
        mx("g", 5, 1)
        mx("m", 5, 1)
        finish(5, 1)
        widen_mom(7)
        mx("g", 2, 1)
        mx("m", 2, 1)
        finish(2, 1)
        turn("m", 4, "vs")
        quant("m", 4)
        mx("g", 4, 1)
        mx("m", 4, 1)
        finish(4, 1)
        widen_mom(1)
        widen_mom(6)
        mx("g", 0, 1)
        mx("m", 0, 1)
        finish(0, 1)
        mx("g", 3, 1)
        mx("m", 3, 1)
        finish(3, 1)
        turn("m", 7, "ss")
        quant("m", 7)
        turn("m", 1, "vs")
        quant("m", 1)
        mx("g", 7, 0)
        mx("m", 7, 0)
        finish(7, 0)
        turn("m", 6, "vs")
        quant("m", 6)
        mx("g", 7, 1)
        mx("m", 7, 1)
        finish(7, 1)
        mx("g", 1, 1)
        mx("m", 1, 1)
        finish(1, 1)
        mx("g", 6, 0)
        mx("m", 6, 0)
        finish(6, 0)
        mx("g", 6, 1)
        mx("m", 6, 1)
        finish(6, 1)
        mx("g", 4, 0)
        mx("m", 4, 0)
        finish(4, 0)
        mx("g", 1, 0)
        mx("m", 1, 0)
        finish(1, 0)
